import numpy as np
import ml_dtypes

BF16 = ml_dtypes.bfloat16


def bf(x):
    return np.asarray(x, np.float32).astype(BF16)


def f32(x):
    return np.asarray(x, np.float32)


def f64(x):
    return np.asarray(x).astype(np.float64)


def striped(idx):
    return np.concatenate([l.reshape(-1, 16).T for l in idx])


def rows(idx, k):
    return np.tile(np.repeat(idx, 16, axis=0), (k // (16 * 8), 1))


def look(tab, idx):
    return np.take_along_axis(f64(tab), rows(idx, len(tab)), axis=1)


K, S, V, N, M = 256, 2048, 1536, 1536, 128


def setup_inputs():
    return {"tab": f32(np.random.standard_normal((K, S))), "pos": f32(np.random.standard_normal((K, V))), "w": bf(np.random.standard_normal((K, M)) / np.sqrt(K)), "offs": striped(np.stack([np.random.permutation(S)[:N] for _ in range(8)]))}


def reference(tab, pos, w, offs):
    idx = np.stack([g.T.reshape(-1) for g in np.split(offs, 8)])
    x = np.maximum(look(tab, idx) - f64(pos) + 0.5, 0.0)
    y = f64(w).T @ x
    return y

@@ -1,0 +1,54 @@
+import concourse.mybir as mybir
+
+P = 128
+ROWS, COLUMNS = 256, 2048
+N = 1536
+M = 128
+PIECE = 512
+BLOCKS, PIECES = ROWS // P, N // PIECE
+LANES = 16
+MARGIN = 0.5
+
+BF16, F32, U16 = mybir.dt.bfloat16, mybir.dt.float32, mybir.dt.uint16
+subtract = mybir.AluOpType.subtract
+relu = mybir.ActivationFunctionType.Relu
+
+FLOPS = 2 * ROWS * M * N
+
+
+def tile_lookup_hinge_sub_none_kernel(tc, tab, pos, w, offs, out):
+    nc = tc.nc
+    with (
+        tc.tile_pool(name="held", bufs=1) as held,
+        tc.tile_pool(name="ring", bufs=3) as ring,
+        tc.psum_pool(name="psum", bufs=1) as psum,
+    ):
+        offsets = held.tile([P, N // LANES], U16, name="offsets")
+        tables = [held.tile([P, COLUMNS], F32, name=f"table{b}") for b in range(BLOCKS)]
+        positives = [[held.tile([P, PIECE], F32, name=f"pos{b}_{j}") for j in range(PIECES)] for b in range(BLOCKS)]
+        weights = held.tile([P, BLOCKS, M], BF16, name="weights")
+        margin = held.tile([P, 1], F32, name="margin")
+        products = [psum.tile([P, PIECE], F32, name=f"product{j}") for j in range(PIECES)]
+
+        nc.sync.dma_start(offsets[:], offs)
+        for b in range(BLOCKS):
+            rows = slice(b * P, (b + 1) * P)
+            nc.sync.dma_start(tables[b][:], tab[rows, :])
+            for j in range(PIECES):
+                nc.sync.dma_start(positives[b][j][:], pos[rows, j * PIECE : (j + 1) * PIECE])
+                if b == 0 and j == 0:
+                    nc.sync.dma_start(weights[:], w.rearrange("(b p) m -> p b m", p=P))
+        nc.vector.memset(margin[:], MARGIN)
+
+        for b in range(BLOCKS):
+            for j in range(PIECES):
+                entries = offsets[:, j * PIECE // LANES : (j + 1) * PIECE // LANES]
+                difference = ring.tile([P, PIECE], F32, name="difference")
+                nc.vector.tensor_tensor(difference[:], tables[b][:].indirect(entries), positives[b][j][:], subtract)
+                x = ring.tile([P, PIECE], BF16, name="x")
+                nc.scalar.activation(x[:], difference[:], relu, bias=margin[:])
+                nc.tensor.matmul(products[j][:], weights[:, b, :], x[:], start=b == 0, stop=b == BLOCKS - 1)
+                if b == BLOCKS - 1:
+                    staged = ring.tile([P, PIECE], F32, name="staged")
+                    nc.scalar.copy(staged[:], products[j][:])
+                    nc.sync.dma_start(out[:, j * PIECE : (j + 1) * PIECE], staged[:])

@@ -6,11 +6,12 @@ N = 1536
 M = 128
 PIECE = 512
 BLOCKS, PIECES = ROWS // P, N // PIECE
+HALF = PIECE // 2
 LANES = 16
 MARGIN = 0.5
 
 BF16, F32, U16 = mybir.dt.bfloat16, mybir.dt.float32, mybir.dt.uint16
-subtract = mybir.AluOpType.subtract
+add, maximum, subtract = mybir.AluOpType.add, mybir.AluOpType.max, mybir.AluOpType.subtract
 relu = mybir.ActivationFunctionType.Relu
 
 FLOPS = 2 * ROWS * M * N
@@ -28,7 +29,10 @@ def tile_lookup_hinge_sub_none_kernel(tc, tab, pos, w, offs, out):
         positives = [[held.tile([P, PIECE], F32, name=f"pos{b}_{j}") for j in range(PIECES)] for b in range(BLOCKS)]
         weights = held.tile([P, BLOCKS, M], BF16, name="weights")
         margin = held.tile([P, 1], F32, name="margin")
-        products = [psum.tile([P, PIECE], F32, name=f"product{j}") for j in range(PIECES)]
+        shares = [[slice(0, PIECE)] for j in range(PIECES - 1)] + [[slice(0, HALF), slice(HALF, PIECE)]]
+        products = [
+            [psum.tile([P, s.stop - s.start], F32, name=f"product{j}_{s.start}") for s in shares[j]] for j in range(PIECES)
+        ]
 
         nc.sync.dma_start(offsets[:], offs)
         for b in range(BLOCKS):
@@ -46,9 +50,19 @@ def tile_lookup_hinge_sub_none_kernel(tc, tab, pos, w, offs, out):
                 difference = ring.tile([P, PIECE], F32, name="difference")
                 nc.vector.tensor_tensor(difference[:], tables[b][:].indirect(entries), positives[b][j][:], subtract)
                 x = ring.tile([P, PIECE], BF16, name="x")
-                nc.scalar.activation(x[:], difference[:], relu, bias=margin[:])
-                nc.tensor.matmul(products[j][:], weights[:, b, :], x[:], start=b == 0, stop=b == BLOCKS - 1)
-                if b == BLOCKS - 1:
-                    staged = ring.tile([P, PIECE], F32, name="staged")
-                    nc.scalar.copy(staged[:], products[j][:])
-                    nc.sync.dma_start(out[:, j * PIECE : (j + 1) * PIECE], staged[:])
+                for k, share in enumerate(shares[j]):
+                    on_vector = b == BLOCKS - 1 and k == 1
+                    product = products[j][k]
+                    if on_vector:
+                        nc.vector.tensor_scalar(x[:, share], difference[:, share], MARGIN, 0.0, add, maximum)
+                    else:
+                        nc.scalar.activation(x[:, share], difference[:, share], relu, bias=margin[:])
+                    nc.tensor.matmul(product[:], weights[:, b, :], x[:, share], start=b == 0, stop=b == BLOCKS - 1)
+                    if b == BLOCKS - 1:
+                        staged = ring.tile([P, share.stop - share.start], F32, name=f"staged{k}")
+                        if on_vector:
+                            nc.vector.tensor_copy(staged[:], product[:])
+                        else:
+                            nc.scalar.copy(staged[:], product[:])
+                        columns = slice(j * PIECE + share.start, j * PIECE + share.stop)
+                        nc.sync.dma_start(out[:, columns], staged[:])

@@ -21,7 +21,7 @@ def tile_lookup_hinge_sub_none_kernel(tc, tab, pos, w, offs, out):
     nc = tc.nc
     with (
         tc.tile_pool(name="held", bufs=1) as held,
-        tc.tile_pool(name="ring", bufs=3) as ring,
+        tc.tile_pool(name="ring", bufs=BLOCKS * PIECES) as ring,
         tc.psum_pool(name="psum", bufs=1) as psum,
     ):
         offsets = held.tile([P, N // LANES], U16, name="offsets")
@@ -40,7 +40,7 @@ def tile_lookup_hinge_sub_none_kernel(tc, tab, pos, w, offs, out):
             nc.sync.dma_start(tables[b][:], tab[rows, :])
             for j in range(PIECES):
                 nc.sync.dma_start(positives[b][j][:], pos[rows, j * PIECE : (j + 1) * PIECE])
-                if b == 0 and j == 0:
+                if b == BLOCKS - 1 and j == 0:
                     nc.sync.dma_start(weights[:], w.rearrange("(b p) m -> p b m", p=P))
         nc.vector.memset(margin[:], MARGIN)
 
@@ -51,16 +51,15 @@ def tile_lookup_hinge_sub_none_kernel(tc, tab, pos, w, offs, out):
                 nc.vector.tensor_tensor(difference[:], tables[b][:].indirect(entries), positives[b][j][:], subtract)
                 x = ring.tile([P, PIECE], BF16, name="x")
                 for k, share in enumerate(shares[j]):
-                    on_vector = b == BLOCKS - 1 and k == 1
                     product = products[j][k]
-                    if on_vector:
+                    if b == BLOCKS - 1 and j == PIECES - 1:
                         nc.vector.tensor_scalar(x[:, share], difference[:, share], MARGIN, 0.0, add, maximum)
                     else:
                         nc.scalar.activation(x[:, share], difference[:, share], relu, bias=margin[:])
                     nc.tensor.matmul(product[:], weights[:, b, :], x[:, share], start=b == 0, stop=b == BLOCKS - 1)
                     if b == BLOCKS - 1:
                         staged = ring.tile([P, share.stop - share.start], F32, name=f"staged{k}")
-                        if on_vector:
+                        if k == 1:
                             nc.vector.tensor_copy(staged[:], product[:])
                         else:
                             nc.scalar.copy(staged[:], product[:])

@@ -34,10 +34,13 @@ def tile_lookup_hinge_sub_none_kernel(tc, tab, pos, w, offs, out):
             [psum.tile([P, s.stop - s.start], F32, name=f"product{j}_{s.start}") for s in shares[j]] for j in range(PIECES)
         ]
 
+        left, right = slice(0, COLUMNS // 2), slice(COLUMNS // 2, COLUMNS)
         nc.sync.dma_start(offsets[:], offs)
         for b in range(BLOCKS):
             rows = slice(b * P, (b + 1) * P)
-            nc.sync.dma_start(tables[b][:], tab[rows, :])
+            first_queue = nc.scalar if b == 0 else nc.sync
+            first_queue.dma_start(tables[b][:, left], tab[rows, left])
+            nc.sync.dma_start(tables[b][:, right], tab[rows, right])
             for j in range(PIECES):
                 nc.sync.dma_start(positives[b][j][:], pos[rows, j * PIECE : (j + 1) * PIECE])
                 if b == BLOCKS - 1 and j == 0:

import concourse.mybir as mybir

P = 128
ROWS, COLUMNS = 256, 2048
N = 1536
M = 128
PIECE = 512
BLOCKS, PIECES = ROWS // P, N // PIECE
HALF = PIECE // 2
LANES = 16
MARGIN = 0.5

BF16, F32, U16 = mybir.dt.bfloat16, mybir.dt.float32, mybir.dt.uint16
add, maximum, subtract = mybir.AluOpType.add, mybir.AluOpType.max, mybir.AluOpType.subtract
relu = mybir.ActivationFunctionType.Relu

FLOPS = 2 * ROWS * M * N


def tile_lookup_hinge_sub_none_kernel(tc, tab, pos, w, offs, out):
    nc = tc.nc
    with (
        tc.tile_pool(name="held", bufs=1) as held,
        tc.tile_pool(name="ring", bufs=BLOCKS * PIECES) as ring,
        tc.psum_pool(name="psum", bufs=1) as psum,
    ):
        offsets = held.tile([P, N // LANES], U16, name="offsets")
        tables = [held.tile([P, COLUMNS], F32, name=f"table{b}") for b in range(BLOCKS)]
        positives = [[held.tile([P, PIECE], F32, name=f"pos{b}_{j}") for j in range(PIECES)] for b in range(BLOCKS)]
        weights = held.tile([P, BLOCKS, M], BF16, name="weights")
        margin = held.tile([P, 1], F32, name="margin")
        shares = [[slice(0, PIECE)] for j in range(PIECES - 1)] + [[slice(0, HALF), slice(HALF, PIECE)]]
        products = [
            [psum.tile([P, s.stop - s.start], F32, name=f"product{j}_{s.start}") for s in shares[j]] for j in range(PIECES)
        ]

        left, right = slice(0, COLUMNS // 2), slice(COLUMNS // 2, COLUMNS)
        nc.sync.dma_start(offsets[:], offs)
        for b in range(BLOCKS):
            rows = slice(b * P, (b + 1) * P)
            first_queue = nc.scalar if b == 0 else nc.sync
            first_queue.dma_start(tables[b][:, left], tab[rows, left])
            nc.sync.dma_start(tables[b][:, right], tab[rows, right])
            for j in range(PIECES):
                nc.sync.dma_start(positives[b][j][:], pos[rows, j * PIECE : (j + 1) * PIECE])
                if b == BLOCKS - 1 and j == 0:
                    nc.sync.dma_start(weights[:], w.rearrange("(b p) m -> p b m", p=P))
        nc.vector.memset(margin[:], MARGIN)

        for b in range(BLOCKS):
            for j in range(PIECES):
                entries = offsets[:, j * PIECE // LANES : (j + 1) * PIECE // LANES]
                difference = ring.tile([P, PIECE], F32, name="difference")
                nc.vector.tensor_tensor(difference[:], tables[b][:].indirect(entries), positives[b][j][:], subtract)
                x = ring.tile([P, PIECE], BF16, name="x")
                for k, share in enumerate(shares[j]):
                    product = products[j][k]
                    if b == BLOCKS - 1 and j == PIECES - 1:
                        nc.vector.tensor_scalar(x[:, share], difference[:, share], MARGIN, 0.0, add, maximum)
                    else:
                        nc.scalar.activation(x[:, share], difference[:, share], relu, bias=margin[:])
                    nc.tensor.matmul(product[:], weights[:, b, :], x[:, share], start=b == 0, stop=b == BLOCKS - 1)
                    if b == BLOCKS - 1:
                        staged = ring.tile([P, share.stop - share.start], F32, name=f"staged{k}")
                        if k == 1:
                            nc.vector.tensor_copy(staged[:], product[:])
                        else:
                            nc.scalar.copy(staged[:], product[:])
                        columns = slice(j * PIECE + share.start, j * PIECE + share.stop)
                        nc.sync.dma_start(out[:, columns], staged[:])
